import numpy as np
import ml_dtypes


def mxq(x, axis, fmt="e4m3"):
    dtype, down = {"e4m3": (ml_dtypes.float8_e4m3fn, 7), "e5m2": (ml_dtypes.float8_e5m2, 14)}[fmt]
    v = np.moveaxis(np.asarray(x, np.float32).astype(ml_dtypes.bfloat16).astype(np.float64), axis, -1)
    blocks = v.reshape(v.shape[:-1] + (-1, 32))
    amax = np.abs(blocks).max(-1, keepdims=True)
    byte = np.maximum(np.where(amax > 0, np.frexp(amax)[1] - 1 + 127, 0) - down, 1)
    scale = np.exp2(byte - 127.0)
    codes = (blocks / scale).astype(np.float32).astype(dtype).astype(np.float64)
    return np.moveaxis((codes * scale).reshape(v.shape), -1, axis)


WIDE = False


def mx_kscale(k):
    if not WIDE:
        return np.ones(k)
    levels = np.array([10, -10, 5, -5, 0])
    if k % 512:
        return np.exp2(np.random.permutation(np.resize(levels, k // 32))).repeat(32)
    a = np.empty((k // 512, 16))
    for p in range(k // 512):
        a[p, :8] = np.random.permutation(np.resize(levels, 8))
        for g in range(8):
            far = levels[np.abs(levels - a[p, g]) >= 10]
            a[p, g + 8] = far[np.random.randint(len(far))]
    return np.exp2(a.ravel()).repeat(32)


def f64(x):
    return np.asarray(x).astype(np.float64)


def striped(idx):
    return np.tile(idx.reshape(-1, 16).T, (8, 1)).astype(np.uint16)


def unstriped(offs):
    return offs[:16].T.reshape(-1).astype(np.int64)


E2M1 = np.array([0.0, 0.5, 1.0, 1.5, 2.0, 3.0, 4.0, 6.0, -0.0, -0.5, -1.0, -1.5, -2.0, -3.0, -4.0, -6.0])


def pack_weight(w, fmt):
    k, n = w.shape
    w = f64(np.asarray(w, np.float32).astype(ml_dtypes.bfloat16)).reshape(k // 32, 32, n)
    amax = np.abs(w).max(1)
    if fmt == "e4m3":
        byte = np.frexp(amax)[1] - 1 + 127 - 7
    else:
        mant, ex = np.frexp(amax / 6.0)
        byte = np.where(mant > 0.5, ex, ex - 1) + 127
    byte = np.clip(np.where(amax > 0, byte, 1), 1, 254)
    scaled = (w * np.exp2(127.0 - byte)[:, None, :]).reshape(k, n).astype(np.float32)
    by_word = np.ascontiguousarray(scaled.reshape(k // 512, 128, 4, n).transpose(0, 1, 3, 2))
    if fmt == "e4m3":
        words = by_word.astype(ml_dtypes.float8_e4m3fn).view(np.uint8)
    else:
        c = by_word.astype(ml_dtypes.float4_e2m1fn).view(np.uint8) & 0xF
        words = (c[..., 0::2] | (c[..., 1::2] << 4)).reshape(k // 512, 128, 2 * n)
    return np.ascontiguousarray(words), np.ascontiguousarray(byte.astype(np.uint8).reshape(k // 512, 16, n))


def unpack_weight(words, scales, fmt):
    g, _, n = scales.shape
    words = np.ascontiguousarray(words).reshape(g, 128, n, -1)
    if fmt == "e4m3":
        vals = words.view(ml_dtypes.float8_e4m3fn).astype(np.float64)
    else:
        nib = np.empty((g, 128, n, 4), np.uint8)
        nib[..., 0::2] = words & 0xF
        nib[..., 1::2] = words >> 4
        vals = E2M1[nib]
    vals = vals * np.repeat(np.exp2(scales.astype(np.float64) - 127.0), 8, axis=1)[..., None]
    return vals.transpose(0, 1, 3, 2).reshape(g * 512, n)


K, T, E, C, N = 1024, 1024, 8, 128, 256
TOP = 3
PAD = 64
K8 = 512


def by_expert(wq, xq):
    return np.concatenate([wq[e].T @ xq[:, e * C:(e + 1) * C] for e in range(E)], axis=1)


def setup_inputs():
    n = np.random.standard_normal
    s = mx_kscale(K)[:, None]
    slot_token = np.empty(E * C, np.int64); pos = np.tile(E * C + np.arange(T) % PAD, (TOP, 1)); taken = np.zeros(T, np.int64)
    liked = np.random.randn(T)
    for e in np.random.permutation(E):
        free = np.flatnonzero(taken < TOP); pick = np.random.permutation(free[np.argsort(-(liked[free] + np.random.gumbel(size=free.size)))[:C]]); slot_token[e * C:(e + 1) * C] = pick
        pos[taken[pick], pick] = e * C + np.arange(C); taken[pick] += 1
    g = np.random.uniform(0.2, 0.8, (TOP, T))
    w = n((E, K, N)) / np.sqrt(K) / s[None]
    w8 = [pack_weight(m[:K8], "e4m3") for m in w]
    w4 = [pack_weight(m[K8:], "e2m1") for m in w]
    return {
        "xT": (n((K, T)) * s).astype(np.float32),
        "w8_words": np.stack([m[0] for m in w8]),
        "w8_scales": np.stack([m[1] for m in w8]),
        "w4_words": np.stack([m[0] for m in w4]),
        "w4_scales": np.stack([m[1] for m in w4]),
        "b": (0.3 * n((N, E))).astype(np.float32),
        "gate": np.stack([np.tile(r, (N, 1)) for r in g]).astype(np.float32),
        "offs": striped(slot_token),
        "pos1": striped(pos[0]),
        "pos2": striped(pos[1]),
        "pos3": striped(pos[2]),
    }


def reference(xT, w8_words, w8_scales, w4_words, w4_scales, b, gate, offs, pos1, pos2, pos3):
    idx = unstriped(offs)
    w = np.stack([np.concatenate([unpack_weight(w8_words[e], w8_scales[e], "e4m3"), unpack_weight(w4_words[e], w4_scales[e], "e2m1")]) for e in range(E)])
    xq = mxq(f64(xT)[:, idx], 0, "e4m3")
    y = by_expert(w, xq)
    y = y + np.repeat(f64(b), C, axis=1)
    y = np.concatenate([y, np.zeros((N, PAD))], axis=1)
    return sum(f64(gate[r]) * y[:, unstriped(p)] for r, p in enumerate((pos1, pos2, pos3)))

@@ -1,0 +1,197 @@
+from contextlib import ExitStack
+
+import concourse.mybir as mybir
+from concourse.masks import make_identity
+
+K, T, E, C, N = 1024, 1024, 8, 128, 256
+TOP = 3
+PAD = 64
+SLOTS = E * C
+FLOPS = 2 * K * N * SLOTS
+
+F32 = mybir.dt.float32
+BF16 = mybir.dt.bfloat16
+I32 = mybir.dt.int32
+U32 = mybir.dt.uint32
+U16 = mybir.dt.uint16
+U8 = mybir.dt.uint8
+FP8X4 = mybir.dt.float8_e4m3fn_x4
+FP4X4 = mybir.dt.float4_e2m1fn_x4
+MULT = mybir.AluOpType.mult
+ADD = mybir.AluOpType.add
+IDENTITY = mybir.ActivationFunctionType.Identity
+
+P = 128
+PACK = 4
+K_PASS = P * PACK
+BANK = 512
+SCALE_ROW = (4, 0)
+X_CHUNKS = (((0, 512, 320), (512, 256, 160), (768, 256, 160)), ((0, 512, 0), (512, 256, 160), (768, 256, 160)))
+SLOT_PIECES = ((0, 512), (512, 256), (768, 256))
+FIRST_PIECES = ((0, 512), (512, 512))
+UNITS = ((0, 0, 512, False), (0, 512, 512, False), (1, 0, 512, False), (1, 512, 256, True), (1, 768, 256, True))
+
+
+def tile_moe_ecr_lin_bias_kernel(
+    tc, xT, w8_words, w8_scales, w4_words, w4_scales, b, gate, offs, pos1, pos2, pos3, out
+):
+    nc = tc.nc
+    with ExitStack() as ctx:
+        keep = ctx.enter_context(tc.tile_pool(name="keep", bufs=1))
+        ring = ctx.enter_context(tc.tile_pool(name="ring", bufs=2))
+        psum = ctx.enter_context(tc.psum_pool(name="psum", bufs=1))
+        banks = [psum.tile([P, BANK], F32, name=f"bank{i}") for i in range(7)]
+
+        offs_t = keep.tile([P, SLOTS // 16], U16, name="offs_t")
+        pos_t = [keep.tile([P, T // 16], U16, name=f"pos_t{r}") for r in range(TOP)]
+
+        w_scales = keep.tile([P, E, N], U8, name="w_scales", align_bytes=64)
+        tok_scales = keep.tile([P, T], U8, name="tok_scales", align_bytes=64)
+        nc.vector.memset(w_scales[:].bitcast(I32), 0)
+        nc.vector.memset(tok_scales[:].bitcast(I32), 0)
+        y = [keep.tile([P, SLOTS + PAD], F32, name=f"y{h}") for h in range(2)]
+        for h in range(2):
+            nc.vector.memset(y[h][:, SLOTS:], 0.0)
+        ident = keep.tile([P, P], F32, name="ident")
+        make_identity(nc, ident[:])
+
+        raw = {}
+        for a in range(2):
+            rows = xT[a * K_PASS : (a + 1) * K_PASS, :].rearrange("(p j) t -> p j t", j=PACK)
+            for t0, width, share in X_CHUNKS[a]:
+                raw[a, t0] = keep.tile([P, PACK, width], F32, name=f"raw{a}_{t0}")
+                nc.sync.dma_start(out=raw[a, t0][:], in_=rows[:, :, t0 : t0 + width])
+            if a == 0:
+                nc.sync.dma_start(offs_t[:], offs)
+        w8_rows = w8_words.rearrange("e a p n r -> p (e a) (n r)")
+        w4_rows = w4_words.rearrange("e a p m -> p (e a) m")
+        w8 = [keep.tile([P, E, 4 * P], U8, name=f"w8_{h}", align_bytes=64) for h in range(2)]
+        w4 = [keep.tile([P, E, 2 * P], U8, name=f"w4_{h}", align_bytes=64) for h in range(2)]
+
+        def load_weights(h):
+            nc.sync.dma_start(out=w8[h][:].bitcast(I32), in_=w8_rows[:, :, 4 * P * h : 4 * P * (h + 1)].bitcast(I32))
+            nc.sync.dma_start(out=w4[h][:].bitcast(I32), in_=w4_rows[:, :, 2 * P * h : 2 * P * (h + 1)].bitcast(I32))
+
+        load_weights(0)
+        for src, row0 in ((w8_scales, SCALE_ROW[0]), (w4_scales, SCALE_ROW[1])):
+            rows = src.rearrange("e a q n -> q (e a) n")
+            for r in range(4):
+                nc.sync.dma_start(out=w_scales[row0 + r : P : 32, :, :].bitcast(I32), in_=rows[r:16:4, :, :].bitcast(I32))
+        bias = keep.tile([P, 2, E], F32, name="bias")
+        nc.sync.dma_start(out=bias[:], in_=b.rearrange("(h p) e -> p h e", p=P))
+        gates = [keep.tile([P, T], F32, name=f"gate{r}") for r in range(TOP)]
+        for r, pos in enumerate((pos1, pos2, pos3)):
+            nc.sync.dma_start(pos_t[r][:], pos)
+            nc.sync.dma_start(out=gates[r][:], in_=gate[r, 0:P, :])
+        load_weights(1)
+
+        tok_words = [keep.tile([P, T], U32, name=f"tok_words{a}", align_bytes=64) for a in range(2)]
+
+        def interleave(copy, grouped, src, c0, c1):
+            copy(
+                out=grouped[:, c0:c1, :].rearrange("p (c i) j -> p c j i", i=4),
+                in_=src[:, :, c0:c1].rearrange("p j (c i) -> p c j i", i=4),
+            )
+
+        def quantize_pass(a):
+            for t0, width, share in X_CHUNKS[a]:
+                grouped = keep.tile([P, width, PACK], BF16, name=f"grouped{a}_{t0}", align_bytes=64)
+                if share > 0:
+                    interleave(nc.vector.tensor_copy, grouped, raw[a, t0], 0, share)
+                if share < width:
+                    interleave(nc.scalar.copy, grouped, raw[a, t0], share, width)
+                nc.vector.quantize_mx(
+                    out=tok_words[a][:, t0 : t0 + width].bitcast(FP8X4),
+                    scales=tok_scales[SCALE_ROW[a] : P, t0 : t0 + width],
+                    in_=grouped[:].rearrange("p t j -> p (t j)"),
+                )
+
+        def gather(name, window, dtype, s0, width):
+            got = keep.tile([P, width], dtype, name=f"{name}_{s0}", align_bytes=64)
+            nc.vector.tensor_copy(got[:], window[:].indirect(offs_t[:, s0 // 16 : (s0 + width) // 16]))
+            return [got[:, c : c + C] for c in range(0, width, C)], got
+
+        quantize_pass(0)
+        slot_words0 = []
+        for s0, width in FIRST_PIECES:
+            slot_words0.extend(gather("slot_words0", tok_words[0], U32, s0, width)[0])
+        quantize_pass(1)
+
+        slot_words1 = []
+        slot_scales = []
+
+        def multiply(h, s0, width, on_vector, acc):
+            for c in range(0, width, C):
+                e = (s0 + c) // C
+                scales, col = slot_scales[e]
+                cols = slice(P * h, P * (h + 1))
+                nc.tensor.matmul_mx(
+                    out=acc[:, c : c + C],
+                    lhsT=w8[h][:, e, :].bitcast(FP8X4),
+                    lhsT_scale=w_scales[SCALE_ROW[0] : P, e, cols],
+                    rhs=slot_words0[e].bitcast(FP8X4),
+                    rhs_scale=scales[SCALE_ROW[0] : P, col : col + C],
+                    start=True,
+                    stop=False,
+                )
+                nc.tensor.matmul_mx(
+                    out=acc[:, c : c + C],
+                    lhsT=w4[h][:, e, :].bitcast(FP4X4),
+                    lhsT_scale=w_scales[SCALE_ROW[1] : P, e, cols],
+                    rhs=slot_words1[e].bitcast(FP8X4),
+                    rhs_scale=scales[SCALE_ROW[1] : P, col : col + C],
+                    start=False,
+                    stop=True,
+                )
+            e0, count = s0 // C, width // C
+            if on_vector:
+                nc.vector.tensor_tensor(
+                    y[h][:, s0 : s0 + width].rearrange("p (e c) -> p e c", c=C),
+                    acc[:, 0:width].rearrange("p (e c) -> p e c", c=C),
+                    bias[:, h, e0 : e0 + count].unsqueeze(2).to_broadcast([P, count, C]),
+                    ADD,
+                )
+            else:
+                for i in range(count):
+                    nc.scalar.activation(
+                        y[h][:, s0 + i * C : s0 + (i + 1) * C],
+                        acc[:, i * C : (i + 1) * C],
+                        IDENTITY,
+                        bias=bias[:, h, e0 + i : e0 + i + 1],
+                    )
+
+        for i, (s0, width) in enumerate(SLOT_PIECES):
+            slot_words1.extend(gather("slot_words1", tok_words[1], U32, s0, width)[0])
+            scales = gather("slot_scales", tok_scales, U8, s0, width)[1]
+            slot_scales.extend([(scales, c) for c in range(0, width, C)])
+            multiply(0, s0, width, s0 + width == SLOTS, banks[i % 3])
+        for s0 in range(0, SLOTS, BANK):
+            multiply(1, s0, BANK, False, banks[3 + s0 // BANK])
+
+        for u, (h, t0, width, on_vector) in enumerate(UNITS):
+            terms = []
+            for r in range(TOP):
+                term = ring.tile([P, width], F32, name=f"term{r}", bufs=3)
+                looked_up = y[h][:].indirect(pos_t[r][:, t0 // 16 : (t0 + width) // 16])
+                nc.vector.tensor_tensor(term[:], looked_up, gates[r][:, t0 : t0 + width], MULT)
+                terms.append(term)
+            result = ring.tile([P, width], F32, name="result", bufs=6)
+            if on_vector:
+                partial = ring.tile([P, width], F32, name="partial")
+                nc.vector.tensor_tensor(partial[:], terms[0][:], terms[1][:], ADD)
+                nc.vector.tensor_tensor(result[:], partial[:], terms[2][:], ADD)
+            else:
+                turned = banks[4 - u % 2]
+                for c in range(0, width, P):
+                    for r in range(TOP):
+                        nc.tensor.matmul(
+                            turned[:, c : c + P], terms[r][:, c : c + P], ident[:],
+                            start=(r == 0), stop=(r == TOP - 1), is_transpose=True,
+                        )
+                summed = ring.tile([P, width], F32, name="summed")
+                nc.scalar.copy(summed[:], turned[:, 0:width])
+                back = banks[5 + u % 2]
+                for c in range(0, width, P):
+                    nc.tensor.transpose(back[:, c : c + P], summed[:, c : c + P], ident[:])
+                nc.scalar.copy(result[:], back[:, 0:width])
+            nc.sync.dma_start(out=out[P * h : P * (h + 1), t0 : t0 + width], in_=result[:])

@@ -26,10 +26,11 @@ PACK = 4
 K_PASS = P * PACK
 BANK = 512
 SCALE_ROW = (4, 0)
-X_CHUNKS = (((0, 512, 320), (512, 256, 160), (768, 256, 160)), ((0, 512, 0), (512, 256, 160), (768, 256, 160)))
-SLOT_PIECES = ((0, 512), (512, 256), (768, 256))
+X_CHUNKS = (((0, 512, 352), (512, 256, 160), (768, 256, 160)), ((0, 256, 0), (256, 256, 0), (512, 256, 64), (768, 256, 192)))
+X_LOADS = (((0, 512), (512, 256), (768, 256)), ((0, 256), (256, 256), (512, 256), (768, 256)))
+SLOT_PIECES = ((0, 512), (512, 256), (768, 128), (896, 128))
 FIRST_PIECES = ((0, 512), (512, 512))
-UNITS = ((0, 0, 512, False), (0, 512, 512, False), (1, 0, 512, False), (1, 512, 256, True), (1, 768, 256, True))
+UNITS = ((0, 0, 512, False), (0, 512, 512, False), (1, 0, 512, False), (1, 512, 256, False), (1, 768, 256, True))
 
 
 def tile_moe_ecr_lin_bias_kernel(
@@ -40,7 +41,7 @@ def tile_moe_ecr_lin_bias_kernel(
         keep = ctx.enter_context(tc.tile_pool(name="keep", bufs=1))
         ring = ctx.enter_context(tc.tile_pool(name="ring", bufs=2))
         psum = ctx.enter_context(tc.psum_pool(name="psum", bufs=1))
-        banks = [psum.tile([P, BANK], F32, name=f"bank{i}") for i in range(7)]
+        banks = [psum.tile([P, BANK], F32, name=f"bank{i}") for i in range(8)]
 
         offs_t = keep.tile([P, SLOTS // 16], U16, name="offs_t")
         pos_t = [keep.tile([P, T // 16], U16, name=f"pos_t{r}") for r in range(TOP)]
@@ -58,32 +59,48 @@ def tile_moe_ecr_lin_bias_kernel(
         raw = {}
         for a in range(2):
             rows = xT[a * K_PASS : (a + 1) * K_PASS, :].rearrange("(p j) t -> p j t", j=PACK)
-            for t0, width, share in X_CHUNKS[a]:
-                raw[a, t0] = keep.tile([P, PACK, width], F32, name=f"raw{a}_{t0}")
-                nc.sync.dma_start(out=raw[a, t0][:], in_=rows[:, :, t0 : t0 + width])
+            for t0, width in X_LOADS[a]:
+                loaded = keep.tile([P, PACK, width], F32, name=f"raw{a}_{t0}")
+                nc.sync.dma_start(out=loaded[:], in_=rows[:, :, t0 : t0 + width])
+                for c0, piece, share in X_CHUNKS[a]:
+                    if t0 <= c0 < t0 + width:
+                        raw[a, c0] = loaded[:, :, c0 - t0 : c0 - t0 + piece]
             if a == 0:
                 nc.sync.dma_start(offs_t[:], offs)
         w8_rows = w8_words.rearrange("e a p n r -> p (e a) (n r)")
         w4_rows = w4_words.rearrange("e a p m -> p (e a) m")
-        w8 = [keep.tile([P, E, 4 * P], U8, name=f"w8_{h}", align_bytes=64) for h in range(2)]
-        w4 = [keep.tile([P, E, 2 * P], U8, name=f"w4_{h}", align_bytes=64) for h in range(2)]
+        w8, w4 = {}, {}
 
-        def load_weights(h):
-            nc.sync.dma_start(out=w8[h][:].bitcast(I32), in_=w8_rows[:, :, 4 * P * h : 4 * P * (h + 1)].bitcast(I32))
-            nc.sync.dma_start(out=w4[h][:].bitcast(I32), in_=w4_rows[:, :, 2 * P * h : 2 * P * (h + 1)].bitcast(I32))
+        def load_weights(h, e0, count):
+            experts = slice(e0, e0 + count)
+            t8 = keep.tile([P, count, 4 * P], U8, name=f"w8_{h}_{e0}", align_bytes=64)
+            t4 = keep.tile([P, count, 2 * P], U8, name=f"w4_{h}_{e0}", align_bytes=64)
+            nc.sync.dma_start(out=t8[:].bitcast(I32), in_=w8_rows[:, experts, 4 * P * h : 4 * P * (h + 1)].bitcast(I32))
+            nc.sync.dma_start(out=t4[:].bitcast(I32), in_=w4_rows[:, experts, 2 * P * h : 2 * P * (h + 1)].bitcast(I32))
+            for i in range(count):
+                w8[h, e0 + i] = t8[:, i, :]
+                w4[h, e0 + i] = t4[:, i, :]
 
-        load_weights(0)
         for src, row0 in ((w8_scales, SCALE_ROW[0]), (w4_scales, SCALE_ROW[1])):
             rows = src.rearrange("e a q n -> q (e a) n")
             for r in range(4):
                 nc.sync.dma_start(out=w_scales[row0 + r : P : 32, :, :].bitcast(I32), in_=rows[r:16:4, :, :].bitcast(I32))
+        load_weights(0, 0, E // 2)
         bias = keep.tile([P, 2, E], F32, name="bias")
         nc.sync.dma_start(out=bias[:], in_=b.rearrange("(h p) e -> p h e", p=P))
-        gates = [keep.tile([P, T], F32, name=f"gate{r}") for r in range(TOP)]
+        load_weights(0, E // 2, E // 2)
         for r, pos in enumerate((pos1, pos2, pos3)):
             nc.sync.dma_start(pos_t[r][:], pos)
-            nc.sync.dma_start(out=gates[r][:], in_=gate[r, 0:P, :])
-        load_weights(1)
+        gates = {}
+
+        def load_gates(t0):
+            for r in range(TOP):
+                gates[r, t0] = keep.tile([P, BANK], F32, name=f"gate{r}_{t0}")
+                nc.sync.dma_start(out=gates[r, t0][:], in_=gate[r, 0:P, t0 : t0 + BANK])
+
+        load_gates(0)
+        load_weights(1, 0, E)
+        load_gates(BANK)
 
         tok_words = [keep.tile([P, T], U32, name=f"tok_words{a}", align_bytes=64) for a in range(2)]
 
@@ -127,7 +144,7 @@ def tile_moe_ecr_lin_bias_kernel(
                 cols = slice(P * h, P * (h + 1))
                 nc.tensor.matmul_mx(
                     out=acc[:, c : c + C],
-                    lhsT=w8[h][:, e, :].bitcast(FP8X4),
+                    lhsT=w8[h, e].bitcast(FP8X4),
                     lhsT_scale=w_scales[SCALE_ROW[0] : P, e, cols],
                     rhs=slot_words0[e].bitcast(FP8X4),
                     rhs_scale=scales[SCALE_ROW[0] : P, col : col + C],
@@ -136,7 +153,7 @@ def tile_moe_ecr_lin_bias_kernel(
                 )
                 nc.tensor.matmul_mx(
                     out=acc[:, c : c + C],
-                    lhsT=w4[h][:, e, :].bitcast(FP4X4),
+                    lhsT=w4[h, e].bitcast(FP4X4),
                     lhsT_scale=w_scales[SCALE_ROW[1] : P, e, cols],
                     rhs=slot_words1[e].bitcast(FP8X4),
                     rhs_scale=scales[SCALE_ROW[1] : P, col : col + C],
@@ -161,19 +178,19 @@ def tile_moe_ecr_lin_bias_kernel(
                     )
 
         for i, (s0, width) in enumerate(SLOT_PIECES):
-            slot_words1.extend(gather("slot_words1", tok_words[1], U32, s0, width)[0])
             scales = gather("slot_scales", tok_scales, U8, s0, width)[1]
             slot_scales.extend([(scales, c) for c in range(0, width, C)])
-            multiply(0, s0, width, s0 + width == SLOTS, banks[i % 3])
+            slot_words1.extend(gather("slot_words1", tok_words[1], U32, s0, width)[0])
+            multiply(0, s0, width, s0 + width == SLOTS, banks[i])
         for s0 in range(0, SLOTS, BANK):
-            multiply(1, s0, BANK, False, banks[3 + s0 // BANK])
+            multiply(1, s0, BANK, False, banks[4 + s0 // BANK])
 
         for u, (h, t0, width, on_vector) in enumerate(UNITS):
             terms = []
             for r in range(TOP):
-                term = ring.tile([P, width], F32, name=f"term{r}", bufs=3)
+                term = ring.tile([P, width], F32, name=f"term{r}", bufs=5)
                 looked_up = y[h][:].indirect(pos_t[r][:, t0 // 16 : (t0 + width) // 16])
-                nc.vector.tensor_tensor(term[:], looked_up, gates[r][:, t0 : t0 + width], MULT)
+                nc.vector.tensor_tensor(term[:], looked_up, gates[r, t0 // BANK * BANK][:, t0 % BANK : t0 % BANK + width], MULT)
                 terms.append(term)
             result = ring.tile([P, width], F32, name="result", bufs=6)
             if on_vector:
@@ -181,17 +198,18 @@ def tile_moe_ecr_lin_bias_kernel(
                 nc.vector.tensor_tensor(partial[:], terms[0][:], terms[1][:], ADD)
                 nc.vector.tensor_tensor(result[:], partial[:], terms[2][:], ADD)
             else:
-                turned = banks[4 - u % 2]
-                for c in range(0, width, P):
-                    for r in range(TOP):
+                blocks = range(width // P)
+                turned = [banks[(5, 4, 0, 1)[j]][:, 0:P] for j in blocks]
+                for r in range(TOP):
+                    for j in blocks:
                         nc.tensor.matmul(
-                            turned[:, c : c + P], terms[r][:, c : c + P], ident[:],
+                            turned[j], terms[r][:, j * P : (j + 1) * P], ident[:],
                             start=(r == 0), stop=(r == TOP - 1), is_transpose=True,
                         )
-                summed = ring.tile([P, width], F32, name="summed")
-                nc.scalar.copy(summed[:], turned[:, 0:width])
-                back = banks[5 + u % 2]
-                for c in range(0, width, P):
-                    nc.tensor.transpose(back[:, c : c + P], summed[:, c : c + P], ident[:])
+                back = banks[6 + u % 2]
+                for j in blocks:
+                    summed = ring.tile([P, P], F32, name="summed", bufs=8)
+                    nc.scalar.copy(summed[:], turned[j])
+                    nc.tensor.transpose(back[:, j * P : (j + 1) * P], summed[:], ident[:])
                 nc.scalar.copy(result[:], back[:, 0:width])
             nc.sync.dma_start(out=out[P * h : P * (h + 1), t0 : t0 + width], in_=result[:])

@@ -26,8 +26,8 @@ PACK = 4
 K_PASS = P * PACK
 BANK = 512
 SCALE_ROW = (4, 0)
-X_CHUNKS = (((0, 512, 352), (512, 256, 160), (768, 256, 160)), ((0, 256, 0), (256, 256, 0), (512, 256, 64), (768, 256, 192)))
-X_LOADS = (((0, 512), (512, 256), (768, 256)), ((0, 256), (256, 256), (512, 256), (768, 256)))
+X_CHUNKS = (((0, 512, 352), (512, 512, 352)), ((0, 256, 0), (256, 256, 0), (512, 256, 256), (768, 256, 160)))
+X_LOADS = (((0, 512), (512, 512)), ((0, 512), (512, 256), (768, 256)))
 SLOT_PIECES = ((0, 512), (512, 256), (768, 128), (896, 128))
 FIRST_PIECES = ((0, 512), (512, 512))
 UNITS = ((0, 0, 512, False), (0, 512, 512, False), (1, 0, 512, False), (1, 512, 256, False), (1, 768, 256, True))
@@ -81,24 +81,25 @@ def tile_moe_ecr_lin_bias_kernel(
                 w8[h, e0 + i] = t8[:, i, :]
                 w4[h, e0 + i] = t4[:, i, :]
 
-        for src, row0 in ((w8_scales, SCALE_ROW[0]), (w4_scales, SCALE_ROW[1])):
+        def load_scales(queue, src, row0):
             rows = src.rearrange("e a q n -> q (e a) n")
             for r in range(4):
-                nc.sync.dma_start(out=w_scales[row0 + r : P : 32, :, :].bitcast(I32), in_=rows[r:16:4, :, :].bitcast(I32))
-        load_weights(0, 0, E // 2)
-        bias = keep.tile([P, 2, E], F32, name="bias")
-        nc.sync.dma_start(out=bias[:], in_=b.rearrange("(h p) e -> p h e", p=P))
-        load_weights(0, E // 2, E // 2)
-        for r, pos in enumerate((pos1, pos2, pos3)):
-            nc.sync.dma_start(pos_t[r][:], pos)
+                queue.dma_start(out=w_scales[row0 + r : P : 32, :, :].bitcast(I32), in_=rows[r:16:4, :, :].bitcast(I32))
+
         gates = {}
 
         def load_gates(t0):
-            for r in range(TOP):
-                gates[r, t0] = keep.tile([P, BANK], F32, name=f"gate{r}_{t0}")
-                nc.sync.dma_start(out=gates[r, t0][:], in_=gate[r, 0:P, t0 : t0 + BANK])
+            gates[t0] = keep.tile([P, TOP, BANK], F32, name=f"gates{t0}")
+            nc.sync.dma_start(out=gates[t0][:], in_=gate[:, 0:P, t0 : t0 + BANK].rearrange("r p t -> p r t"))
 
+        load_scales(nc.gpsimd, w8_scales, SCALE_ROW[0])
+        load_weights(0, 0, E)
+        load_scales(nc.sync, w4_scales, SCALE_ROW[1])
+        bias = keep.tile([P, 2, E], F32, name="bias")
+        nc.sync.dma_start(out=bias[:], in_=b.rearrange("(h p) e -> p h e", p=P))
         load_gates(0)
+        for r, pos in enumerate((pos1, pos2, pos3)):
+            nc.sync.dma_start(pos_t[r][:], pos)
         load_weights(1, 0, E)
         load_gates(BANK)
 
@@ -190,7 +191,7 @@ def tile_moe_ecr_lin_bias_kernel(
             for r in range(TOP):
                 term = ring.tile([P, width], F32, name=f"term{r}", bufs=5)
                 looked_up = y[h][:].indirect(pos_t[r][:, t0 // 16 : (t0 + width) // 16])
-                nc.vector.tensor_tensor(term[:], looked_up, gates[r, t0 // BANK * BANK][:, t0 % BANK : t0 % BANK + width], MULT)
+                nc.vector.tensor_tensor(term[:], looked_up, gates[t0 // BANK * BANK][:, r, t0 % BANK : t0 % BANK + width], MULT)
                 terms.append(term)
             result = ring.tile([P, width], F32, name="result", bufs=6)
             if on_vector:

@@ -41,7 +41,7 @@ def tile_moe_ecr_lin_bias_kernel(
         keep = ctx.enter_context(tc.tile_pool(name="keep", bufs=1))
         ring = ctx.enter_context(tc.tile_pool(name="ring", bufs=2))
         psum = ctx.enter_context(tc.psum_pool(name="psum", bufs=1))
-        banks = [psum.tile([P, BANK], F32, name=f"bank{i}") for i in range(8)]
+        banks = [psum.tile([P, BANK], F32, name=f"bank{i}") for i in range(6)]
 
         offs_t = keep.tile([P, SLOTS // 16], U16, name="offs_t")
         pos_t = [keep.tile([P, T // 16], U16, name=f"pos_t{r}") for r in range(TOP)]
@@ -81,10 +81,13 @@ def tile_moe_ecr_lin_bias_kernel(
                 w8[h, e0 + i] = t8[:, i, :]
                 w4[h, e0 + i] = t4[:, i, :]
 
-        def load_scales(queue, src, row0):
-            rows = src.rearrange("e a q n -> q (e a) n")
-            for r in range(4):
-                queue.dma_start(out=w_scales[row0 + r : P : 32, :, :].bitcast(I32), in_=rows[r:16:4, :, :].bitcast(I32))
+        def load_scale_rows(first, last):
+            for i in range(first, last):
+                a, r = divmod(i, 4)
+                rows = (w8_scales, w4_scales)[a].rearrange("e a q n -> q (e a) n")
+                nc.sync.dma_start(
+                    out=w_scales[SCALE_ROW[a] + r : P : 32, :, :].bitcast(I32), in_=rows[r:16:4, :, :].bitcast(I32)
+                )
 
         gates = {}
 
@@ -92,16 +95,19 @@ def tile_moe_ecr_lin_bias_kernel(
             gates[t0] = keep.tile([P, TOP, BANK], F32, name=f"gates{t0}")
             nc.sync.dma_start(out=gates[t0][:], in_=gate[:, 0:P, t0 : t0 + BANK].rearrange("r p t -> p r t"))
 
-        load_scales(nc.gpsimd, w8_scales, SCALE_ROW[0])
-        load_weights(0, 0, E)
-        load_scales(nc.sync, w4_scales, SCALE_ROW[1])
+        load_scale_rows(0, 3)
+        load_weights(0, 0, E // 2)
+        load_scale_rows(3, 8)
         bias = keep.tile([P, 2, E], F32, name="bias")
         nc.sync.dma_start(out=bias[:], in_=b.rearrange("(h p) e -> p h e", p=P))
+        load_weights(0, E // 2, E // 2)
+        nc.sync.dma_start(pos_t[0][:], pos1)
         load_gates(0)
-        for r, pos in enumerate((pos1, pos2, pos3)):
-            nc.sync.dma_start(pos_t[r][:], pos)
-        load_weights(1, 0, E)
+        nc.sync.dma_start(pos_t[1][:], pos2)
+        nc.sync.dma_start(pos_t[2][:], pos3)
+        load_weights(1, 0, E // 2)
         load_gates(BANK)
+        load_weights(1, E // 2, E // 2)
 
         tok_words = [keep.tile([P, T], U32, name=f"tok_words{a}", align_bytes=64) for a in range(2)]
 
@@ -183,10 +189,11 @@ def tile_moe_ecr_lin_bias_kernel(
             slot_scales.extend([(scales, c) for c in range(0, width, C)])
             slot_words1.extend(gather("slot_words1", tok_words[1], U32, s0, width)[0])
             multiply(0, s0, width, s0 + width == SLOTS, banks[i])
-        for s0 in range(0, SLOTS, BANK):
-            multiply(1, s0, BANK, False, banks[4 + s0 // BANK])
 
         for u, (h, t0, width, on_vector) in enumerate(UNITS):
+            if h == 0:
+                for j in range(4):
+                    multiply(1, (4 * u + j) * C, C, False, banks[j])
             terms = []
             for r in range(TOP):
                 term = ring.tile([P, width], F32, name=f"term{r}", bufs=5)
@@ -200,14 +207,14 @@ def tile_moe_ecr_lin_bias_kernel(
                 nc.vector.tensor_tensor(result[:], partial[:], terms[2][:], ADD)
             else:
                 blocks = range(width // P)
-                turned = [banks[(5, 4, 0, 1)[j]][:, 0:P] for j in blocks]
+                turned = [banks[j][:, 0:P] for j in blocks]
                 for r in range(TOP):
                     for j in blocks:
                         nc.tensor.matmul(
                             turned[j], terms[r][:, j * P : (j + 1) * P], ident[:],
                             start=(r == 0), stop=(r == TOP - 1), is_transpose=True,
                         )
-                back = banks[6 + u % 2]
+                back = banks[4 + u % 2]
                 for j in blocks:
                     summed = ring.tile([P, P], F32, name="summed", bufs=8)
                     nc.scalar.copy(summed[:], turned[j])

@@ -25,12 +25,18 @@ P = 128
 PACK = 4
 K_PASS = P * PACK
 BANK = 512
-SCALE_ROW = (4, 0)
-X_CHUNKS = (((0, 512, 352), (512, 512, 352)), ((0, 256, 0), (256, 256, 0), (512, 256, 256), (768, 256, 160)))
+LIST_ROWS = 16
+QUADRANT = 32
+ROWS_PER_QUADRANT = 4
+SCALE_ROW = (ROWS_PER_QUADRANT, 0)
+LINE = 4
+
 X_LOADS = (((0, 512), (512, 512)), ((0, 512), (512, 256), (768, 256)))
-SLOT_PIECES = ((0, 512), (512, 256), (768, 128), (896, 128))
-FIRST_PIECES = ((0, 512), (512, 512))
-UNITS = ((0, 0, 512, False), (0, 512, 512, False), (1, 0, 512, False), (1, 512, 256, False), (1, 768, 256, True))
+X_PIECES = (((0, 512, 352), (512, 512, 352)), ((0, 256, 0), (256, 256, 0), (512, 256, 256), (768, 256, 160)))
+PASS0_GATHERS = ((0, 512), (512, 512))
+PASS1_GATHERS = ((0, 512), (512, 256), (768, 128), (896, 128))
+STRETCHES = ((0, 0, 512, False), (0, 512, 512, False), (1, 0, 512, False), (1, 512, 256, False), (1, 768, 256, True))
+EARLY_SCALE_LOADS = 3
 
 
 def tile_moe_ecr_lin_bias_kernel(
@@ -41,32 +47,37 @@ def tile_moe_ecr_lin_bias_kernel(
         keep = ctx.enter_context(tc.tile_pool(name="keep", bufs=1))
         ring = ctx.enter_context(tc.tile_pool(name="ring", bufs=2))
         psum = ctx.enter_context(tc.psum_pool(name="psum", bufs=1))
-        banks = [psum.tile([P, BANK], F32, name=f"bank{i}") for i in range(6)]
+        banks = [psum.tile([P, BANK], F32, name=f"bank{i}") for i in range(2 * TOP)]
 
-        offs_t = keep.tile([P, SLOTS // 16], U16, name="offs_t")
-        pos_t = [keep.tile([P, T // 16], U16, name=f"pos_t{r}") for r in range(TOP)]
+        offs_t = keep.tile([P, SLOTS // LIST_ROWS], U16, name="offs_t")
+        pos_t = [keep.tile([P, T // LIST_ROWS], U16, name=f"pos_t{r}") for r in range(TOP)]
 
         w_scales = keep.tile([P, E, N], U8, name="w_scales", align_bytes=64)
         tok_scales = keep.tile([P, T], U8, name="tok_scales", align_bytes=64)
         nc.vector.memset(w_scales[:].bitcast(I32), 0)
         nc.vector.memset(tok_scales[:].bitcast(I32), 0)
-        y = [keep.tile([P, SLOTS + PAD], F32, name=f"y{h}") for h in range(2)]
-        for h in range(2):
+        y = [keep.tile([P, SLOTS + PAD], F32, name=f"y{h}") for h in range(N // P)]
+        for h in range(N // P):
             nc.vector.memset(y[h][:, SLOTS:], 0.0)
         ident = keep.tile([P, P], F32, name="ident")
         make_identity(nc, ident[:])
 
+        per_partition = T // P
+        gate_cols = keep.tile([P, TOP, per_partition], F32, name="gate_cols")
+        nc.sync.dma_start(out=gate_cols[:], in_=gate[:, 0, :].rearrange("r (p i) -> p r i", p=P))
+
         raw = {}
-        for a in range(2):
-            rows = xT[a * K_PASS : (a + 1) * K_PASS, :].rearrange("(p j) t -> p j t", j=PACK)
+        for a in range(K // K_PASS):
+            x_rows = xT[a * K_PASS : (a + 1) * K_PASS, :].rearrange("(p j) t -> p j t", j=PACK)
             for t0, width in X_LOADS[a]:
                 loaded = keep.tile([P, PACK, width], F32, name=f"raw{a}_{t0}")
-                nc.sync.dma_start(out=loaded[:], in_=rows[:, :, t0 : t0 + width])
-                for c0, piece, share in X_CHUNKS[a]:
-                    if t0 <= c0 < t0 + width:
-                        raw[a, c0] = loaded[:, :, c0 - t0 : c0 - t0 + piece]
+                nc.sync.dma_start(out=loaded[:], in_=x_rows[:, :, t0 : t0 + width])
+                for first, tokens, share in X_PIECES[a]:
+                    if t0 <= first < t0 + width:
+                        raw[a, first] = loaded[:, :, first - t0 : first - t0 + tokens]
             if a == 0:
                 nc.sync.dma_start(offs_t[:], offs)
+
         w8_rows = w8_words.rearrange("e a p n r -> p (e a) (n r)")
         w4_rows = w4_words.rearrange("e a p m -> p (e a) m")
         w8, w4 = {}, {}
@@ -83,42 +94,34 @@ def tile_moe_ecr_lin_bias_kernel(
 
         def load_scale_rows(first, last):
             for i in range(first, last):
-                a, r = divmod(i, 4)
-                rows = (w8_scales, w4_scales)[a].rearrange("e a q n -> q (e a) n")
+                a, row = divmod(i, ROWS_PER_QUADRANT)
+                scale_rows = (w8_scales, w4_scales)[a].rearrange("e a q n -> q (e a) n")
                 nc.sync.dma_start(
-                    out=w_scales[SCALE_ROW[a] + r : P : 32, :, :].bitcast(I32), in_=rows[r:16:4, :, :].bitcast(I32)
+                    out=w_scales[SCALE_ROW[a] + row : P : QUADRANT, :, :].bitcast(I32),
+                    in_=scale_rows[row : 4 * ROWS_PER_QUADRANT : ROWS_PER_QUADRANT, :, :].bitcast(I32),
                 )
 
-        gates = {}
-
-        def load_gates(t0):
-            gates[t0] = keep.tile([P, TOP, BANK], F32, name=f"gates{t0}")
-            nc.sync.dma_start(out=gates[t0][:], in_=gate[:, 0:P, t0 : t0 + BANK].rearrange("r p t -> p r t"))
-
-        load_scale_rows(0, 3)
+        load_scale_rows(0, EARLY_SCALE_LOADS)
         load_weights(0, 0, E // 2)
-        load_scale_rows(3, 8)
-        bias = keep.tile([P, 2, E], F32, name="bias")
+        load_scale_rows(EARLY_SCALE_LOADS, 2 * ROWS_PER_QUADRANT)
+        bias = keep.tile([P, N // P, E], F32, name="bias")
         nc.sync.dma_start(out=bias[:], in_=b.rearrange("(h p) e -> p h e", p=P))
         load_weights(0, E // 2, E // 2)
-        nc.sync.dma_start(pos_t[0][:], pos1)
-        load_gates(0)
-        nc.sync.dma_start(pos_t[1][:], pos2)
-        nc.sync.dma_start(pos_t[2][:], pos3)
+        for pos_tile, pos in zip(pos_t, (pos1, pos2, pos3)):
+            nc.sync.dma_start(pos_tile[:], pos)
         load_weights(1, 0, E // 2)
-        load_gates(BANK)
         load_weights(1, E // 2, E // 2)
 
-        tok_words = [keep.tile([P, T], U32, name=f"tok_words{a}", align_bytes=64) for a in range(2)]
+        tok_words = [keep.tile([P, T], U32, name=f"tok_words{a}", align_bytes=64) for a in range(K // K_PASS)]
 
         def interleave(copy, grouped, src, c0, c1):
             copy(
-                out=grouped[:, c0:c1, :].rearrange("p (c i) j -> p c j i", i=4),
-                in_=src[:, :, c0:c1].rearrange("p j (c i) -> p c j i", i=4),
+                out=grouped[:, c0:c1, :].rearrange("p (c i) j -> p c j i", i=LINE),
+                in_=src[:, :, c0:c1].rearrange("p j (c i) -> p c j i", i=LINE),
             )
 
         def quantize_pass(a):
-            for t0, width, share in X_CHUNKS[a]:
+            for t0, width, share in X_PIECES[a]:
                 grouped = keep.tile([P, width, PACK], BF16, name=f"grouped{a}_{t0}", align_bytes=64)
                 if share > 0:
                     interleave(nc.vector.tensor_copy, grouped, raw[a, t0], 0, share)
@@ -130,31 +133,45 @@ def tile_moe_ecr_lin_bias_kernel(
                     in_=grouped[:].rearrange("p t j -> p (t j)"),
                 )
 
-        def gather(name, window, dtype, s0, width):
+        def gather_slots(name, window, dtype, s0, width):
             got = keep.tile([P, width], dtype, name=f"{name}_{s0}", align_bytes=64)
-            nc.vector.tensor_copy(got[:], window[:].indirect(offs_t[:, s0 // 16 : (s0 + width) // 16]))
-            return [got[:, c : c + C] for c in range(0, width, C)], got
+            entries = offs_t[:, s0 // LIST_ROWS : (s0 + width) // LIST_ROWS]
+            nc.vector.tensor_copy(got[:], window[:].indirect(entries))
+            return [got[:, c : c + C] for c in range(0, width, C)]
 
         quantize_pass(0)
         slot_words0 = []
-        for s0, width in FIRST_PIECES:
-            slot_words0.extend(gather("slot_words0", tok_words[0], U32, s0, width)[0])
+        for s0, width in PASS0_GATHERS:
+            slot_words0.extend(gather_slots("slot_words0", tok_words[0], U32, s0, width))
         quantize_pass(1)
+
+        gates = [keep.tile([P, T], F32, name=f"gate{r}") for r in range(TOP)]
+        per_bank = BANK // P
+        for r in range(TOP):
+            for half in range(per_partition // per_bank):
+                bank = banks[2 * r + half]
+                i0 = per_bank * half
+                for i in range(per_bank):
+                    column = gate_cols[:, r, i0 + i : i0 + i + 1]
+                    nc.tensor.transpose(bank[:, i * P : (i + 1) * P], column.to_broadcast([P, P]), ident[:])
+                nc.scalar.copy(
+                    gates[r][:].rearrange("m (p i) -> m p i", p=P)[:, :, i0 : i0 + per_bank],
+                    bank[:].rearrange("m (i p) -> m p i", p=P),
+                )
 
         slot_words1 = []
         slot_scales = []
 
-        def multiply(h, s0, width, on_vector, acc):
+        def multiply(h, s0, width, bias_on_vector, acc):
             for c in range(0, width, C):
                 e = (s0 + c) // C
-                scales, col = slot_scales[e]
                 cols = slice(P * h, P * (h + 1))
                 nc.tensor.matmul_mx(
                     out=acc[:, c : c + C],
                     lhsT=w8[h, e].bitcast(FP8X4),
                     lhsT_scale=w_scales[SCALE_ROW[0] : P, e, cols],
                     rhs=slot_words0[e].bitcast(FP8X4),
-                    rhs_scale=scales[SCALE_ROW[0] : P, col : col + C],
+                    rhs_scale=slot_scales[e][SCALE_ROW[0] : P, :],
                     start=True,
                     stop=False,
                 )
@@ -163,12 +180,12 @@ def tile_moe_ecr_lin_bias_kernel(
                     lhsT=w4[h, e].bitcast(FP4X4),
                     lhsT_scale=w_scales[SCALE_ROW[1] : P, e, cols],
                     rhs=slot_words1[e].bitcast(FP8X4),
-                    rhs_scale=scales[SCALE_ROW[1] : P, col : col + C],
+                    rhs_scale=slot_scales[e][SCALE_ROW[1] : P, :],
                     start=False,
                     stop=True,
                 )
             e0, count = s0 // C, width // C
-            if on_vector:
+            if bias_on_vector:
                 nc.vector.tensor_tensor(
                     y[h][:, s0 : s0 + width].rearrange("p (e c) -> p e c", c=C),
                     acc[:, 0:width].rearrange("p (e c) -> p e c", c=C),
@@ -184,24 +201,23 @@ def tile_moe_ecr_lin_bias_kernel(
                         bias=bias[:, h, e0 + i : e0 + i + 1],
                     )
 
-        for i, (s0, width) in enumerate(SLOT_PIECES):
-            scales = gather("slot_scales", tok_scales, U8, s0, width)[1]
-            slot_scales.extend([(scales, c) for c in range(0, width, C)])
-            slot_words1.extend(gather("slot_words1", tok_words[1], U32, s0, width)[0])
+        for i, (s0, width) in enumerate(PASS1_GATHERS):
+            slot_scales.extend(gather_slots("slot_scales", tok_scales, U8, s0, width))
+            slot_words1.extend(gather_slots("slot_words1", tok_words[1], U32, s0, width))
             multiply(0, s0, width, s0 + width == SLOTS, banks[i])
 
-        for u, (h, t0, width, on_vector) in enumerate(UNITS):
+        for u, (h, t0, width, add_on_vector) in enumerate(STRETCHES):
             if h == 0:
-                for j in range(4):
-                    multiply(1, (4 * u + j) * C, C, False, banks[j])
+                for j in range(E // 2):
+                    multiply(1, (E // 2 * u + j) * C, C, False, banks[j])
             terms = []
             for r in range(TOP):
-                term = ring.tile([P, width], F32, name=f"term{r}", bufs=5)
-                looked_up = y[h][:].indirect(pos_t[r][:, t0 // 16 : (t0 + width) // 16])
-                nc.vector.tensor_tensor(term[:], looked_up, gates[t0 // BANK * BANK][:, r, t0 % BANK : t0 % BANK + width], MULT)
+                term = ring.tile([P, width], F32, name=f"term{r}", bufs=len(STRETCHES))
+                looked_up = y[h][:].indirect(pos_t[r][:, t0 // LIST_ROWS : (t0 + width) // LIST_ROWS])
+                nc.vector.tensor_tensor(term[:], looked_up, gates[r][:, t0 : t0 + width], MULT)
                 terms.append(term)
-            result = ring.tile([P, width], F32, name="result", bufs=6)
-            if on_vector:
+            result = ring.tile([P, width], F32, name="result", bufs=len(STRETCHES))
+            if add_on_vector:
                 partial = ring.tile([P, width], F32, name="partial")
                 nc.vector.tensor_tensor(partial[:], terms[0][:], terms[1][:], ADD)
                 nc.vector.tensor_tensor(result[:], partial[:], terms[2][:], ADD)
@@ -214,9 +230,9 @@ def tile_moe_ecr_lin_bias_kernel(
                             turned[j], terms[r][:, j * P : (j + 1) * P], ident[:],
                             start=(r == 0), stop=(r == TOP - 1), is_transpose=True,
                         )
-                back = banks[4 + u % 2]
+                back = banks[per_bank + u % 2]
                 for j in blocks:
-                    summed = ring.tile([P, P], F32, name="summed", bufs=8)
+                    summed = ring.tile([P, P], F32, name="summed", bufs=2 * per_bank)
                     nc.scalar.copy(summed[:], turned[j])
                     nc.tensor.transpose(back[:, j * P : (j + 1) * P], summed[:], ident[:])
                 nc.scalar.copy(result[:], back[:, 0:width])

from contextlib import ExitStack

import concourse.mybir as mybir
from concourse.masks import make_identity

K, T, E, C, N = 1024, 1024, 8, 128, 256
TOP = 3
PAD = 64
SLOTS = E * C
FLOPS = 2 * K * N * SLOTS

F32 = mybir.dt.float32
BF16 = mybir.dt.bfloat16
I32 = mybir.dt.int32
U32 = mybir.dt.uint32
U16 = mybir.dt.uint16
U8 = mybir.dt.uint8
FP8X4 = mybir.dt.float8_e4m3fn_x4
FP4X4 = mybir.dt.float4_e2m1fn_x4
MULT = mybir.AluOpType.mult
ADD = mybir.AluOpType.add
IDENTITY = mybir.ActivationFunctionType.Identity

P = 128
PACK = 4
K_PASS = P * PACK
BANK = 512
LIST_ROWS = 16
QUADRANT = 32
ROWS_PER_QUADRANT = 4
SCALE_ROW = (ROWS_PER_QUADRANT, 0)
LINE = 4

X_LOADS = (((0, 512), (512, 512)), ((0, 512), (512, 256), (768, 256)))
X_PIECES = (((0, 512, 352), (512, 512, 352)), ((0, 256, 0), (256, 256, 0), (512, 256, 256), (768, 256, 160)))
PASS0_GATHERS = ((0, 512), (512, 512))
PASS1_GATHERS = ((0, 512), (512, 256), (768, 128), (896, 128))
STRETCHES = ((0, 0, 512, False), (0, 512, 512, False), (1, 0, 512, False), (1, 512, 256, False), (1, 768, 256, True))
EARLY_SCALE_LOADS = 3


def tile_moe_ecr_lin_bias_kernel(
    tc, xT, w8_words, w8_scales, w4_words, w4_scales, b, gate, offs, pos1, pos2, pos3, out
):
    nc = tc.nc
    with ExitStack() as ctx:
        keep = ctx.enter_context(tc.tile_pool(name="keep", bufs=1))
        ring = ctx.enter_context(tc.tile_pool(name="ring", bufs=2))
        psum = ctx.enter_context(tc.psum_pool(name="psum", bufs=1))
        banks = [psum.tile([P, BANK], F32, name=f"bank{i}") for i in range(2 * TOP)]

        offs_t = keep.tile([P, SLOTS // LIST_ROWS], U16, name="offs_t")
        pos_t = [keep.tile([P, T // LIST_ROWS], U16, name=f"pos_t{r}") for r in range(TOP)]

        w_scales = keep.tile([P, E, N], U8, name="w_scales", align_bytes=64)
        tok_scales = keep.tile([P, T], U8, name="tok_scales", align_bytes=64)
        nc.vector.memset(w_scales[:].bitcast(I32), 0)
        nc.vector.memset(tok_scales[:].bitcast(I32), 0)
        y = [keep.tile([P, SLOTS + PAD], F32, name=f"y{h}") for h in range(N // P)]
        for h in range(N // P):
            nc.vector.memset(y[h][:, SLOTS:], 0.0)
        ident = keep.tile([P, P], F32, name="ident")
        make_identity(nc, ident[:])

        per_partition = T // P
        gate_cols = keep.tile([P, TOP, per_partition], F32, name="gate_cols")
        nc.sync.dma_start(out=gate_cols[:], in_=gate[:, 0, :].rearrange("r (p i) -> p r i", p=P))

        raw = {}
        for a in range(K // K_PASS):
            x_rows = xT[a * K_PASS : (a + 1) * K_PASS, :].rearrange("(p j) t -> p j t", j=PACK)
            for t0, width in X_LOADS[a]:
                loaded = keep.tile([P, PACK, width], F32, name=f"raw{a}_{t0}")
                nc.sync.dma_start(out=loaded[:], in_=x_rows[:, :, t0 : t0 + width])
                for first, tokens, share in X_PIECES[a]:
                    if t0 <= first < t0 + width:
                        raw[a, first] = loaded[:, :, first - t0 : first - t0 + tokens]
            if a == 0:
                nc.sync.dma_start(offs_t[:], offs)

        w8_rows = w8_words.rearrange("e a p n r -> p (e a) (n r)")
        w4_rows = w4_words.rearrange("e a p m -> p (e a) m")
        w8, w4 = {}, {}

        def load_weights(h, e0, count):
            experts = slice(e0, e0 + count)
            t8 = keep.tile([P, count, 4 * P], U8, name=f"w8_{h}_{e0}", align_bytes=64)
            t4 = keep.tile([P, count, 2 * P], U8, name=f"w4_{h}_{e0}", align_bytes=64)
            nc.sync.dma_start(out=t8[:].bitcast(I32), in_=w8_rows[:, experts, 4 * P * h : 4 * P * (h + 1)].bitcast(I32))
            nc.sync.dma_start(out=t4[:].bitcast(I32), in_=w4_rows[:, experts, 2 * P * h : 2 * P * (h + 1)].bitcast(I32))
            for i in range(count):
                w8[h, e0 + i] = t8[:, i, :]
                w4[h, e0 + i] = t4[:, i, :]

        def load_scale_rows(first, last):
            for i in range(first, last):
                a, row = divmod(i, ROWS_PER_QUADRANT)
                scale_rows = (w8_scales, w4_scales)[a].rearrange("e a q n -> q (e a) n")
                nc.sync.dma_start(
                    out=w_scales[SCALE_ROW[a] + row : P : QUADRANT, :, :].bitcast(I32),
                    in_=scale_rows[row : 4 * ROWS_PER_QUADRANT : ROWS_PER_QUADRANT, :, :].bitcast(I32),
                )

        load_scale_rows(0, EARLY_SCALE_LOADS)
        load_weights(0, 0, E // 2)
        load_scale_rows(EARLY_SCALE_LOADS, 2 * ROWS_PER_QUADRANT)
        bias = keep.tile([P, N // P, E], F32, name="bias")
        nc.sync.dma_start(out=bias[:], in_=b.rearrange("(h p) e -> p h e", p=P))
        load_weights(0, E // 2, E // 2)
        for pos_tile, pos in zip(pos_t, (pos1, pos2, pos3)):
            nc.sync.dma_start(pos_tile[:], pos)
        load_weights(1, 0, E // 2)
        load_weights(1, E // 2, E // 2)

        tok_words = [keep.tile([P, T], U32, name=f"tok_words{a}", align_bytes=64) for a in range(K // K_PASS)]

        def interleave(copy, grouped, src, c0, c1):
            copy(
                out=grouped[:, c0:c1, :].rearrange("p (c i) j -> p c j i", i=LINE),
                in_=src[:, :, c0:c1].rearrange("p j (c i) -> p c j i", i=LINE),
            )

        def quantize_pass(a):
            for t0, width, share in X_PIECES[a]:
                grouped = keep.tile([P, width, PACK], BF16, name=f"grouped{a}_{t0}", align_bytes=64)
                if share > 0:
                    interleave(nc.vector.tensor_copy, grouped, raw[a, t0], 0, share)
                if share < width:
                    interleave(nc.scalar.copy, grouped, raw[a, t0], share, width)
                nc.vector.quantize_mx(
                    out=tok_words[a][:, t0 : t0 + width].bitcast(FP8X4),
                    scales=tok_scales[SCALE_ROW[a] : P, t0 : t0 + width],
                    in_=grouped[:].rearrange("p t j -> p (t j)"),
                )

        def gather_slots(name, window, dtype, s0, width):
            got = keep.tile([P, width], dtype, name=f"{name}_{s0}", align_bytes=64)
            entries = offs_t[:, s0 // LIST_ROWS : (s0 + width) // LIST_ROWS]
            nc.vector.tensor_copy(got[:], window[:].indirect(entries))
            return [got[:, c : c + C] for c in range(0, width, C)]

        quantize_pass(0)
        slot_words0 = []
        for s0, width in PASS0_GATHERS:
            slot_words0.extend(gather_slots("slot_words0", tok_words[0], U32, s0, width))
        quantize_pass(1)

        gates = [keep.tile([P, T], F32, name=f"gate{r}") for r in range(TOP)]
        per_bank = BANK // P
        for r in range(TOP):
            for half in range(per_partition // per_bank):
                bank = banks[2 * r + half]
                i0 = per_bank * half
                for i in range(per_bank):
                    column = gate_cols[:, r, i0 + i : i0 + i + 1]
                    nc.tensor.transpose(bank[:, i * P : (i + 1) * P], column.to_broadcast([P, P]), ident[:])
                nc.scalar.copy(
                    gates[r][:].rearrange("m (p i) -> m p i", p=P)[:, :, i0 : i0 + per_bank],
                    bank[:].rearrange("m (i p) -> m p i", p=P),
                )

        slot_words1 = []
        slot_scales = []

        def multiply(h, s0, width, bias_on_vector, acc):
            for c in range(0, width, C):
                e = (s0 + c) // C
                cols = slice(P * h, P * (h + 1))
                nc.tensor.matmul_mx(
                    out=acc[:, c : c + C],
                    lhsT=w8[h, e].bitcast(FP8X4),
                    lhsT_scale=w_scales[SCALE_ROW[0] : P, e, cols],
                    rhs=slot_words0[e].bitcast(FP8X4),
                    rhs_scale=slot_scales[e][SCALE_ROW[0] : P, :],
                    start=True,
                    stop=False,
                )
                nc.tensor.matmul_mx(
                    out=acc[:, c : c + C],
                    lhsT=w4[h, e].bitcast(FP4X4),
                    lhsT_scale=w_scales[SCALE_ROW[1] : P, e, cols],
                    rhs=slot_words1[e].bitcast(FP8X4),
                    rhs_scale=slot_scales[e][SCALE_ROW[1] : P, :],
                    start=False,
                    stop=True,
                )
            e0, count = s0 // C, width // C
            if bias_on_vector:
                nc.vector.tensor_tensor(
                    y[h][:, s0 : s0 + width].rearrange("p (e c) -> p e c", c=C),
                    acc[:, 0:width].rearrange("p (e c) -> p e c", c=C),
                    bias[:, h, e0 : e0 + count].unsqueeze(2).to_broadcast([P, count, C]),
                    ADD,
                )
            else:
                for i in range(count):
                    nc.scalar.activation(
                        y[h][:, s0 + i * C : s0 + (i + 1) * C],
                        acc[:, i * C : (i + 1) * C],
                        IDENTITY,
                        bias=bias[:, h, e0 + i : e0 + i + 1],
                    )

        for i, (s0, width) in enumerate(PASS1_GATHERS):
            slot_scales.extend(gather_slots("slot_scales", tok_scales, U8, s0, width))
            slot_words1.extend(gather_slots("slot_words1", tok_words[1], U32, s0, width))
            multiply(0, s0, width, s0 + width == SLOTS, banks[i])

        for u, (h, t0, width, add_on_vector) in enumerate(STRETCHES):
            if h == 0:
                for j in range(E // 2):
                    multiply(1, (E // 2 * u + j) * C, C, False, banks[j])
            terms = []
            for r in range(TOP):
                term = ring.tile([P, width], F32, name=f"term{r}", bufs=len(STRETCHES))
                looked_up = y[h][:].indirect(pos_t[r][:, t0 // LIST_ROWS : (t0 + width) // LIST_ROWS])
                nc.vector.tensor_tensor(term[:], looked_up, gates[r][:, t0 : t0 + width], MULT)
                terms.append(term)
            result = ring.tile([P, width], F32, name="result", bufs=len(STRETCHES))
            if add_on_vector:
                partial = ring.tile([P, width], F32, name="partial")
                nc.vector.tensor_tensor(partial[:], terms[0][:], terms[1][:], ADD)
                nc.vector.tensor_tensor(result[:], partial[:], terms[2][:], ADD)
            else:
                blocks = range(width // P)
                turned = [banks[j][:, 0:P] for j in blocks]
                for r in range(TOP):
                    for j in blocks:
                        nc.tensor.matmul(
                            turned[j], terms[r][:, j * P : (j + 1) * P], ident[:],
                            start=(r == 0), stop=(r == TOP - 1), is_transpose=True,
                        )
                back = banks[per_bank + u % 2]
                for j in blocks:
                    summed = ring.tile([P, P], F32, name="summed", bufs=2 * per_bank)
                    nc.scalar.copy(summed[:], turned[j])
                    nc.tensor.transpose(back[:, j * P : (j + 1) * P], summed[:], ident[:])
                nc.scalar.copy(result[:], back[:, 0:width])
            nc.sync.dma_start(out=out[P * h : P * (h + 1), t0 : t0 + width], in_=result[:])
